import numpy as np
import ml_dtypes


def mxq(x, axis, fmt="e4m3"):
    dtype, down = {"e4m3": (ml_dtypes.float8_e4m3fn, 7), "e5m2": (ml_dtypes.float8_e5m2, 14)}[fmt]
    v = np.moveaxis(np.asarray(x, np.float32).astype(ml_dtypes.bfloat16).astype(np.float64), axis, -1)
    blocks = v.reshape(v.shape[:-1] + (-1, 32))
    amax = np.abs(blocks).max(-1, keepdims=True)
    byte = np.maximum(np.where(amax > 0, np.frexp(amax)[1] - 1 + 127, 0) - down, 1)
    scale = np.exp2(byte - 127.0)
    codes = (blocks / scale).astype(np.float32).astype(dtype).astype(np.float64)
    return np.moveaxis((codes * scale).reshape(v.shape), -1, axis)


WIDE = False


def mx_kscale(k):
    if not WIDE:
        return np.ones(k)
    levels = np.array([10, -10, 5, -5, 0])
    if k % 512:
        return np.exp2(np.random.permutation(np.resize(levels, k // 32))).repeat(32)
    a = np.empty((k // 512, 16))
    for p in range(k // 512):
        a[p, :8] = np.random.permutation(np.resize(levels, 8))
        for g in range(8):
            far = levels[np.abs(levels - a[p, g]) >= 10]
            a[p, g + 8] = far[np.random.randint(len(far))]
    return np.exp2(a.ravel()).repeat(32)


def f64(x):
    return np.asarray(x).astype(np.float64)


def striped8(idx):
    return np.asarray(idx).reshape(8, -1, 16).transpose(0, 2, 1).reshape(128, -1).astype(np.uint16)


def unstriped8(offs):
    return offs.reshape(8, 16, -1).transpose(0, 2, 1).reshape(8, -1).astype(np.int64)


def pick8(x, idx, run):
    r = np.arange(len(x))
    return x[r[:, None], idx[r % (8 * run) // run]]


E2M1 = np.array([0.0, 0.5, 1.0, 1.5, 2.0, 3.0, 4.0, 6.0, -0.0, -0.5, -1.0, -1.5, -2.0, -3.0, -4.0, -6.0])


def pack_weight(w, fmt):
    k, n = w.shape
    w = f64(np.asarray(w, np.float32).astype(ml_dtypes.bfloat16)).reshape(k // 32, 32, n)
    amax = np.abs(w).max(1)
    if fmt == "e4m3":
        byte = np.frexp(amax)[1] - 1 + 127 - 7
    else:
        mant, ex = np.frexp(amax / 6.0)
        byte = np.where(mant > 0.5, ex, ex - 1) + 127
    byte = np.clip(np.where(amax > 0, byte, 1), 1, 254)
    scaled = (w * np.exp2(127.0 - byte)[:, None, :]).reshape(k, n).astype(np.float32)
    by_word = np.ascontiguousarray(scaled.reshape(k // 512, 128, 4, n).transpose(0, 1, 3, 2))
    if fmt == "e4m3":
        words = by_word.astype(ml_dtypes.float8_e4m3fn).view(np.uint8)
    else:
        c = by_word.astype(ml_dtypes.float4_e2m1fn).view(np.uint8) & 0xF
        words = (c[..., 0::2] | (c[..., 1::2] << 4)).reshape(k // 512, 128, 2 * n)
    return np.ascontiguousarray(words), np.ascontiguousarray(byte.astype(np.uint8).reshape(k // 512, 16, n))


def unpack_weight(words, scales, fmt):
    g, _, n = scales.shape
    words = np.ascontiguousarray(words).reshape(g, 128, n, -1)
    if fmt == "e4m3":
        vals = words.view(ml_dtypes.float8_e4m3fn).astype(np.float64)
    else:
        nib = np.empty((g, 128, n, 4), np.uint8)
        nib[..., 0::2] = words & 0xF
        nib[..., 1::2] = words >> 4
        vals = E2M1[nib]
    vals = vals * np.repeat(np.exp2(scales.astype(np.float64) - 127.0), 8, axis=1)[..., None]
    return vals.transpose(0, 1, 3, 2).reshape(g * 512, n)


D, V, Q, I = 512, 2048, 128, 512


def setup_inputs():
    n = np.random.standard_normal
    idx = np.stack([np.random.permutation(V)[:I] for _ in range(8)])
    fd = mx_kscale(D)
    vocp = pack_weight(n((D, V)) / fd[:, None], "e4m3")
    return {
        "hid": (n((D, Q)) * 0.7 / np.sqrt(D) * fd[:, None]).astype(np.float32),
        "voc_words": vocp[0],
        "voc_scales": vocp[1],
        "lpo": (np.random.uniform(-8.2, -7.2, (Q, I))).astype(np.float32),
        "adv": (1.0 * n((Q, I))).astype(np.float32),
        "old": (0.5 * n((Q, V))).astype(np.float32),
        "offs": striped8(idx),
    }


def reference(hid, voc_words, voc_scales, lpo, adv, old, offs):
    idx = unstriped8(offs)
    vocu = unpack_weight(voc_words, voc_scales, "e4m3")
    hidq = mxq(f64(hid), 0, "e4m3")
    a = hidq.T @ vocu
    p = np.exp(a)
    z = np.sum(p, axis=1, keepdims=True)
    r = np.exp(pick8(a, idx, 16) - np.log(z) - f64(lpo))
    dz = np.sum(f64(adv) * r * (-1.0), axis=1, keepdims=True) / z
    e1 = f64(adv) * r
    s1 = np.zeros((Q, V))
    s1[np.arange(Q)[:, None], idx[np.arange(Q) % 128 // 16]] = e1
    da = dz * p + s1
    y = da * 1.0 + f64(old)
    return y

@@ -1,0 +1,145 @@
+from contextlib import ExitStack
+
+import concourse.mybir as mybir
+
+D, V, Q, I = 512, 2048, 128, 512
+FLOPS = 2 * D * V * Q
+
+F32 = mybir.dt.float32
+BF16 = mybir.dt.bfloat16
+I32 = mybir.dt.int32
+U32 = mybir.dt.uint32
+U16 = mybir.dt.uint16
+U8 = mybir.dt.uint8
+FP8X4 = mybir.dt.float8_e4m3fn_x4
+ALU = mybir.AluOpType
+ACT = mybir.ActivationFunctionType
+
+P = 128
+PACK = 4
+N = 512
+CHUNKS = V // N
+HALF = V // 2
+OUT_WIDTHS = (512, 512, 512, 256, 256)
+
+
+def tile_attend_bpolicyratio_heads_kernel(tc, hid, voc_words, voc_scales, lpo, adv, old, offs, out):
+    nc = tc.nc
+    with ExitStack() as ctx:
+        keep = ctx.enter_context(tc.tile_pool(name="keep", bufs=1))
+        psum = ctx.enter_context(tc.psum_pool(name="psum", bufs=1))
+
+        offsets = keep.tile([P, I // 16], U16, name="offsets")
+        hid_raw = keep.tile([P, PACK, Q], F32, name="hid_raw")
+        hid_bf = keep.tile([P, Q, PACK], BF16, name="hid_bf", align_bytes=64)
+        hid_codes = keep.tile([P, Q], U32, name="hid_codes", align_bytes=64)
+        hid_scales = keep.tile([P, Q], U8, name="hid_scales", align_bytes=64)
+        voc_planes = keep.tile([P, N], U8, name="voc_planes", align_bytes=64)
+        voc_codes = [keep.tile([P, N], U32, name="voc_codes%d" % c, align_bytes=64) for c in range(CHUNKS)]
+        lpo_sb = keep.tile([P, I], F32, name="lpo_sb")
+        adv_sb = keep.tile([P, I], F32, name="adv_sb")
+        old_sb = [keep.tile([P, HALF], F32, name="old_sb%d" % h) for h in range(2)]
+        scores = keep.tile([P, V], F32, name="scores")
+        probs = keep.tile([P, V], F32, name="probs")
+        placed = keep.tile([P, V], F32, name="placed")
+        picked = keep.tile([P, I], F32, name="picked")
+        ratio = keep.tile([P, I], F32, name="ratio")
+        gain = keep.tile([P, I], F32, name="gain")
+        run_max = keep.tile([P, CHUNKS], F32, name="run_max")
+        neg_max = keep.tile([P, 2], F32, name="neg_max")
+        half_sum = keep.tile([P, 2], F32, name="half_sum")
+        rescale = keep.tile([P, 2], F32, name="rescale")
+        weighted = keep.tile([P, 2], F32, name="weighted")
+        total = keep.tile([P, 1], F32, name="total")
+        inv_total = keep.tile([P, 1], F32, name="inv_total")
+        gain_sum = keep.tile([P, 1], F32, name="gain_sum")
+        coef = keep.tile([P, 2], F32, name="coef")
+
+        nc.vector.memset(voc_planes[:].bitcast(U32), 0)
+        nc.vector.memset(placed[:], 0.0)
+
+        nc.sync.dma_start(out=hid_raw[:], in_=hid.rearrange("(p j) q -> p j q", j=PACK))
+        for g in range(4):
+            nc.scalar.dma_start(
+                out=voc_planes[32 * g : 32 * g + 16, :].bitcast(I32),
+                in_=voc_scales[0][4 * g : 4 * g + 4, :].rearrange("r (c n) -> c r n", c=CHUNKS).bitcast(I32),
+            )
+        words = voc_words[0].rearrange("p n t -> p (n t)")
+        for c in range(CHUNKS):
+            nc.sync.dma_start(
+                out=voc_codes[c][:].bitcast(I32),
+                in_=words[:, c * N * PACK : (c + 1) * N * PACK].bitcast(I32),
+            )
+        nc.sync.dma_start(offsets[:], offs)
+        nc.sync.dma_start(out=lpo_sb[:], in_=lpo)
+        nc.sync.dma_start(out=adv_sb[:], in_=adv)
+        for h in range(2):
+            nc.sync.dma_start(out=old_sb[h][:], in_=old[:, h * HALF : (h + 1) * HALF])
+
+        nc.vector.tensor_copy(out=hid_bf[:], in_=hid_raw[:].rearrange("p j q -> p q j"))
+        nc.vector.quantize_mx(
+            out=hid_codes[:].bitcast(FP8X4),
+            scales=hid_scales[:],
+            in_=hid_bf[:].rearrange("p q j -> p (q j)"),
+        )
+
+        for c in range(CHUNKS):
+            bank = psum.tile([P, N], F32, name="bank%d" % c)
+            nc.tensor.matmul_mx(
+                out=bank[:],
+                lhsT=hid_codes[:].bitcast(FP8X4),
+                lhsT_scale=hid_scales[:],
+                rhs=voc_codes[c][:].bitcast(FP8X4),
+                rhs_scale=voc_planes[4 * c : P, :],
+                start=True,
+                stop=True,
+            )
+            nc.vector.tensor_scalar(
+                out=scores[:, c * N : (c + 1) * N],
+                in0=bank[:],
+                scalar1=1.0,
+                scalar2=None if c == 0 else run_max[:, c - 1 : c],
+                op0=ALU.mult,
+                op1=ALU.max,
+                accum_out=run_max[:, c : c + 1],
+            )
+            if c % 2 == 1:
+                h = c // 2
+                nc.scalar.mul(neg_max[:, h : h + 1], run_max[:, c : c + 1], -1.0)
+                nc.scalar.activation(
+                    out=probs[:, h * HALF : (h + 1) * HALF],
+                    in_=scores[:, h * HALF : (h + 1) * HALF],
+                    func=ACT.Exp,
+                    bias=neg_max[:, h : h + 1],
+                    accum_out=half_sum[:, h : h + 1],
+                )
+
+        nc.vector.tensor_tensor(picked[:], scores[:].indirect(offsets[:]), lpo_sb[:], ALU.subtract)
+        nc.scalar.activation(out=rescale[:], in_=run_max[:, 1:CHUNKS:2], func=ACT.Exp, bias=neg_max[:, 1:2])
+        nc.scalar.activation(out=ratio[:], in_=picked[:], func=ACT.Exp, bias=neg_max[:, 1:2])
+        nc.vector.scalar_tensor_tensor(
+            out=weighted[:], in0=half_sum[:], scalar=1.0, in1=rescale[:], op0=ALU.mult, op1=ALU.mult,
+            accum_out=total[:],
+        )
+        nc.vector.reciprocal(inv_total[:], total[:])
+        nc.vector.scalar_tensor_tensor(
+            out=gain[:], in0=ratio[:], scalar=inv_total[:], in1=adv_sb[:], op0=ALU.mult, op1=ALU.mult,
+            accum_out=gain_sum[:],
+        )
+        nc.vector.tensor_copy(placed[:].indirect(offsets[:]), gain[:])
+        nc.vector.tensor_scalar(
+            out=coef[:], in0=rescale[:], scalar1=gain_sum[:], scalar2=inv_total[:], op0=ALU.mult, op1=ALU.mult
+        )
+
+        c0 = 0
+        for k, w in enumerate(OUT_WIDTHS):
+            h = c0 // HALF
+            dense = keep.tile([P, w], F32, name="dense%d" % k)
+            result = keep.tile([P, w], F32, name="result%d" % k)
+            nc.vector.scalar_tensor_tensor(
+                out=dense[:], in0=probs[:, c0 : c0 + w], scalar=coef[:, h : h + 1],
+                in1=old_sb[h][:, c0 - h * HALF : c0 - h * HALF + w], op0=ALU.mult, op1=ALU.subtract,
+            )
+            nc.vector.tensor_tensor(result[:], placed[:, c0 : c0 + w], dense[:], ALU.subtract)
+            nc.sync.dma_start(out=out[:, c0 : c0 + w], in_=result[:])
+            c0 = c0 + w

@@ -1,6 +1,7 @@
 from contextlib import ExitStack
 
 import concourse.mybir as mybir
+from concourse.masks import make_identity
 
 D, V, Q, I = 512, 2048, 128, 512
 FLOPS = 2 * D * V * Q
@@ -20,7 +21,7 @@ PACK = 4
 N = 512
 CHUNKS = V // N
 HALF = V // 2
-OUT_WIDTHS = (512, 512, 512, 256, 256)
+DIRECT = 256
 
 
 def tile_attend_bpolicyratio_heads_kernel(tc, hid, voc_words, voc_scales, lpo, adv, old, offs, out):
@@ -45,17 +46,20 @@ def tile_attend_bpolicyratio_heads_kernel(tc, hid, voc_words, voc_scales, lpo, a
         picked = keep.tile([P, I], F32, name="picked")
         ratio = keep.tile([P, I], F32, name="ratio")
         gain = keep.tile([P, I], F32, name="gain")
-        run_max = keep.tile([P, CHUNKS], F32, name="run_max")
-        neg_max = keep.tile([P, 2], F32, name="neg_max")
-        half_sum = keep.tile([P, 2], F32, name="half_sum")
-        rescale = keep.tile([P, 2], F32, name="rescale")
-        weighted = keep.tile([P, 2], F32, name="weighted")
+        chunk_max = keep.tile([P, CHUNKS], F32, name="chunk_max")
+        neg_max = keep.tile([P, 3], F32, name="neg_max")
+        group_sum = keep.tile([P, 3], F32, name="group_sum")
+        rescale = keep.tile([P, 3], F32, name="rescale")
+        weighted = keep.tile([P, 3], F32, name="weighted")
         total = keep.tile([P, 1], F32, name="total")
         inv_total = keep.tile([P, 1], F32, name="inv_total")
-        gain_sum = keep.tile([P, 1], F32, name="gain_sum")
-        coef = keep.tile([P, 2], F32, name="coef")
+        neg_share = keep.tile([P, 3], F32, name="neg_share")
+        gain_sum = keep.tile([P, 2], F32, name="gain_sum")
+        coef_part = keep.tile([P, 3], F32, name="coef_part")
+        coef = keep.tile([P, 3], F32, name="coef")
+        identity = keep.tile([P, P], F32, name="identity")
 
-        nc.vector.memset(voc_planes[:].bitcast(U32), 0)
+        make_identity(nc, identity[:])
         nc.vector.memset(placed[:], 0.0)
 
         nc.sync.dma_start(out=hid_raw[:], in_=hid.rearrange("(p j) q -> p j q", j=PACK))
@@ -76,7 +80,11 @@ def tile_attend_bpolicyratio_heads_kernel(tc, hid, voc_words, voc_scales, lpo, a
         for h in range(2):
             nc.sync.dma_start(out=old_sb[h][:], in_=old[:, h * HALF : (h + 1) * HALF])
 
-        nc.vector.tensor_copy(out=hid_bf[:], in_=hid_raw[:].rearrange("p j q -> p q j"))
+        for copy, rows in ((nc.vector.tensor_copy, slice(0, Q // 2)), (nc.scalar.copy, slice(Q // 2, Q))):
+            copy(
+                hid_bf[:, rows, :].rearrange("p (c i) j -> p c j i", i=4),
+                hid_raw[:, :, rows].rearrange("p j (c i) -> p c j i", i=4),
+            )
         nc.vector.quantize_mx(
             out=hid_codes[:].bitcast(FP8X4),
             scales=hid_scales[:],
@@ -84,7 +92,7 @@ def tile_attend_bpolicyratio_heads_kernel(tc, hid, voc_words, voc_scales, lpo, a
         )
 
         for c in range(CHUNKS):
-            bank = psum.tile([P, N], F32, name="bank%d" % c)
+            bank = psum.tile([P, N], F32, name="bank%d" % c, tag="bank%d" % c)
             nc.tensor.matmul_mx(
                 out=bank[:],
                 lhsT=hid_codes[:].bitcast(FP8X4),
@@ -98,48 +106,109 @@ def tile_attend_bpolicyratio_heads_kernel(tc, hid, voc_words, voc_scales, lpo, a
                 out=scores[:, c * N : (c + 1) * N],
                 in0=bank[:],
                 scalar1=1.0,
-                scalar2=None if c == 0 else run_max[:, c - 1 : c],
+                scalar2=None,
                 op0=ALU.mult,
                 op1=ALU.max,
-                accum_out=run_max[:, c : c + 1],
+                accum_out=chunk_max[:, c : c + 1],
             )
-            if c % 2 == 1:
-                h = c // 2
-                nc.scalar.mul(neg_max[:, h : h + 1], run_max[:, c : c + 1], -1.0)
+            if 1 <= c <= 2:
+                g = c - 1
+                nc.vector.tensor_scalar(
+                    out=neg_max[:, g : g + 1], in0=chunk_max[:, g : g + 1], scalar1=-1.0, scalar2=None, op0=ALU.mult
+                )
                 nc.scalar.activation(
-                    out=probs[:, h * HALF : (h + 1) * HALF],
-                    in_=scores[:, h * HALF : (h + 1) * HALF],
-                    func=ACT.Exp,
-                    bias=neg_max[:, h : h + 1],
-                    accum_out=half_sum[:, h : h + 1],
+                    out=probs[:, g * N : (g + 1) * N], in_=scores[:, g * N : (g + 1) * N], func=ACT.Exp,
+                    bias=neg_max[:, g : g + 1], accum_out=group_sum[:, g : g + 1],
                 )
 
+        nc.vector.tensor_reduce(
+            out=neg_max[:, 2:3], in_=chunk_max[:], axis=mybir.AxisListType.X, op=ALU.max, negate=True
+        )
         nc.vector.tensor_tensor(picked[:], scores[:].indirect(offsets[:]), lpo_sb[:], ALU.subtract)
-        nc.scalar.activation(out=rescale[:], in_=run_max[:, 1:CHUNKS:2], func=ACT.Exp, bias=neg_max[:, 1:2])
-        nc.scalar.activation(out=ratio[:], in_=picked[:], func=ACT.Exp, bias=neg_max[:, 1:2])
+        nc.scalar.activation(out=rescale[:], in_=neg_max[:], func=ACT.Exp, bias=neg_max[:, 2:3], scale=-1.0)
+        nc.scalar.activation(
+            out=probs[:, HALF:V], in_=scores[:, HALF:V], func=ACT.Exp,
+            bias=neg_max[:, 2:3], accum_out=group_sum[:, 2:3],
+        )
         nc.vector.scalar_tensor_tensor(
-            out=weighted[:], in0=half_sum[:], scalar=1.0, in1=rescale[:], op0=ALU.mult, op1=ALU.mult,
+            out=weighted[:], in0=group_sum[:], scalar=1.0, in1=rescale[:], op0=ALU.mult, op1=ALU.mult,
             accum_out=total[:],
         )
         nc.vector.reciprocal(inv_total[:], total[:])
-        nc.vector.scalar_tensor_tensor(
-            out=gain[:], in0=ratio[:], scalar=inv_total[:], in1=adv_sb[:], op0=ALU.mult, op1=ALU.mult,
-            accum_out=gain_sum[:],
-        )
-        nc.vector.tensor_copy(placed[:].indirect(offsets[:]), gain[:])
         nc.vector.tensor_scalar(
-            out=coef[:], in0=rescale[:], scalar1=gain_sum[:], scalar2=inv_total[:], op0=ALU.mult, op1=ALU.mult
+            out=neg_share[:], in0=rescale[:], scalar1=inv_total[:], scalar2=-1.0, op0=ALU.mult, op1=ALU.mult
         )
-
-        c0 = 0
-        for k, w in enumerate(OUT_WIDTHS):
-            h = c0 // HALF
-            dense = keep.tile([P, w], F32, name="dense%d" % k)
-            result = keep.tile([P, w], F32, name="result%d" % k)
+        for s in range(2):
+            slots = slice(s * I // 2, (s + 1) * I // 2)
+            nc.scalar.activation(out=ratio[:, slots], in_=picked[:, slots], func=ACT.Exp, bias=neg_max[:, 2:3])
             nc.vector.scalar_tensor_tensor(
-                out=dense[:], in0=probs[:, c0 : c0 + w], scalar=coef[:, h : h + 1],
-                in1=old_sb[h][:, c0 - h * HALF : c0 - h * HALF + w], op0=ALU.mult, op1=ALU.subtract,
+                out=gain[:, slots], in0=ratio[:, slots], scalar=inv_total[:], in1=adv_sb[:, slots],
+                op0=ALU.mult, op1=ALU.mult, accum_out=gain_sum[:, s : s + 1],
             )
-            nc.vector.tensor_tensor(result[:], placed[:, c0 : c0 + w], dense[:], ALU.subtract)
+        nc.scalar.activation(out=coef_part[:], in_=neg_share[:], func=ACT.Copy, scale=gain_sum[:, 0:1])
+        for g in range(3):
+            nc.scalar.activation(
+                out=coef[:, g : g + 1], in_=neg_share[:, g : g + 1], func=ACT.Identity,
+                scale=gain_sum[:, 1:2], bias=coef_part[:, g : g + 1],
+            )
+        nc.vector.tensor_copy(placed[:].indirect(offsets[:]), gain[:])
+
+        def old_cols(c0, w):
+            h = c0 // HALF
+            return old_sb[h][:, c0 - h * HALF : c0 - h * HALF + w]
+
+        def coef_of(c):
+            return coef[:, min(c, 2) : min(c, 2) + 1]
+
+        widths = [N] * (CHUNKS - 1) + [N - DIRECT]
+        turned = []
+        for c in range(CHUNKS):
+            acc = psum.tile([P, widths[c]], F32, name="acc%d" % c)
+            for b in range(widths[c] // P):
+                nc.tensor.matmul(
+                    acc[:, b * P : (b + 1) * P], lhsT=old_cols(c * N + b * P, P), rhs=identity[:],
+                    start=(b == 0), stop=False, is_transpose=True,
+                )
+            turned.append(acc)
+
+        def scale_and_turn(c):
+            blocks = widths[c] // P
+            scaled = keep.tile([P, widths[c]], F32, name="scaled%d" % c)
+            nc.scalar.activation(
+                out=scaled[:], in_=probs[:, c * N : c * N + widths[c]], func=ACT.Copy, scale=coef_of(c)
+            )
+            for b in range(blocks):
+                nc.tensor.matmul(
+                    turned[c][:, b * P : (b + 1) * P], lhsT=scaled[:, b * P : (b + 1) * P], rhs=identity[:],
+                    start=False, stop=(b == blocks - 1), is_transpose=True,
+                )
+
+        def turn_back(c):
+            staged = keep.tile([P, widths[c]], F32, name="staged%d" % c)
+            nc.scalar.copy(staged[:], turned[c][:])
+            back = psum.tile([P, widths[c]], F32, name="back%d" % c, tag="bank%d" % c)
+            for b in range(widths[c] // P):
+                nc.tensor.transpose(back[:, b * P : (b + 1) * P], staged[:, b * P : (b + 1) * P], identity[:])
+            return back
+
+        def finish(dense, c0, w):
+            result = keep.tile([P, w], F32, name="result%d" % c0)
+            nc.vector.tensor_tensor(result[:], dense, placed[:, c0 : c0 + w], ALU.add)
             nc.sync.dma_start(out=out[:, c0 : c0 + w], in_=result[:])
-            c0 = c0 + w
+
+        backs = []
+        scale_and_turn(0)
+        for c in range(1, CHUNKS):
+            scale_and_turn(c)
+            backs.append(turn_back(c - 1))
+        backs.append(turn_back(CHUNKS - 1))
+
+        direct = keep.tile([P, DIRECT], F32, name="direct")
+        nc.vector.scalar_tensor_tensor(
+            out=direct[:], in0=probs[:, V - DIRECT : V], scalar=coef_of(CHUNKS - 1),
+            in1=old_cols(V - DIRECT, DIRECT), op0=ALU.mult, op1=ALU.add,
+        )
+        finish(backs[0][:], 0, N)
+        finish(direct[:], V - DIRECT, DIRECT)
+        for c in range(1, CHUNKS):
+            finish(backs[c][:], c * N, widths[c])

@@ -21,7 +21,7 @@ PACK = 4
 N = 512
 CHUNKS = V // N
 HALF = V // 2
-DIRECT = 256
+TURNED_WIDTHS = (512, 512, 256)
 
 
 def tile_attend_bpolicyratio_heads_kernel(tc, hid, voc_words, voc_scales, lpo, adv, old, offs, out):
@@ -160,9 +160,9 @@ def tile_attend_bpolicyratio_heads_kernel(tc, hid, voc_words, voc_scales, lpo, a
         def coef_of(c):
             return coef[:, min(c, 2) : min(c, 2) + 1]
 
-        widths = [N] * (CHUNKS - 1) + [N - DIRECT]
+        widths = TURNED_WIDTHS
         turned = []
-        for c in range(CHUNKS):
+        for c in range(len(widths)):
             acc = psum.tile([P, widths[c]], F32, name="acc%d" % c)
             for b in range(widths[c] // P):
                 nc.tensor.matmul(
@@ -196,19 +196,25 @@ def tile_attend_bpolicyratio_heads_kernel(tc, hid, voc_words, voc_scales, lpo, a
             nc.vector.tensor_tensor(result[:], dense, placed[:, c0 : c0 + w], ALU.add)
             nc.sync.dma_start(out=out[:, c0 : c0 + w], in_=result[:])
 
-        backs = []
-        scale_and_turn(0)
-        for c in range(1, CHUNKS):
-            scale_and_turn(c)
-            backs.append(turn_back(c - 1))
-        backs.append(turn_back(CHUNKS - 1))
+        def add_on_gpsimd(c0, w):
+            scaled = keep.tile([P, w], F32, name="scaled_at%d" % c0)
+            nc.scalar.activation(out=scaled[:], in_=probs[:, c0 : c0 + w], func=ACT.Copy, scale=coef_of(2))
+            summed = keep.tile([P, w], F32, name="summed_at%d" % c0)
+            nc.gpsimd.tensor_tensor(summed[:], scaled[:], old_cols(c0, w), ALU.add)
+            return summed
 
-        direct = keep.tile([P, DIRECT], F32, name="direct")
-        nc.vector.scalar_tensor_tensor(
-            out=direct[:], in0=probs[:, V - DIRECT : V], scalar=coef_of(CHUNKS - 1),
-            in1=old_cols(V - DIRECT, DIRECT), op0=ALU.mult, op1=ALU.add,
-        )
-        finish(backs[0][:], 0, N)
-        finish(direct[:], V - DIRECT, DIRECT)
-        for c in range(1, CHUNKS):
-            finish(backs[c][:], c * N, widths[c])
+        scale_and_turn(0)
+        scale_and_turn(1)
+        back0 = turn_back(0)
+        summed_a = add_on_gpsimd(1280, 512)
+        scale_and_turn(2)
+        back1 = turn_back(1)
+        summed_b = add_on_gpsimd(1792, 256)
+        back2 = turn_back(2)
+
+        finish(back0[:, 0:256], 0, 256)
+        finish(back0[:, 256:512], 256, 256)
+        finish(back1[:], 512, 512)
+        finish(back2[:], 1024, 256)
+        finish(summed_a[:], 1280, 512)
+        finish(summed_b[:], 1792, 256)

@@ -18,10 +18,21 @@ ACT = mybir.ActivationFunctionType
 
 P = 128
 PACK = 4
+LIST_ROWS = 16
+QUADRANT = 32
+SCALE_ROWS = 4
+LINE = 4
 N = 512
 CHUNKS = V // N
 HALF = V // 2
-TURNED_WIDTHS = (512, 512, 256)
+SCORE_PIECES = ((0, N // 2), (N // 2, N // 2), (N, N), (2 * N, N), (3 * N, N // 2), (3 * N + N // 2, N // 2))
+GROUPS = 3
+LAST_GROUP = GROUPS - 1
+TURNED_WIDTHS = (N, N, N // 2)
+ACC_TAGS = ("acc0", "acc1", "bank0")
+GPSIMD_START = sum(TURNED_WIDTHS)
+GPSIMD_LAST = 256
+GPSIMD_FIRST = V - GPSIMD_START - GPSIMD_LAST
 
 
 def tile_attend_bpolicyratio_heads_kernel(tc, hid, voc_words, voc_scales, lpo, adv, old, offs, out):
@@ -30,12 +41,12 @@ def tile_attend_bpolicyratio_heads_kernel(tc, hid, voc_words, voc_scales, lpo, a
         keep = ctx.enter_context(tc.tile_pool(name="keep", bufs=1))
         psum = ctx.enter_context(tc.psum_pool(name="psum", bufs=1))
 
-        offsets = keep.tile([P, I // 16], U16, name="offsets")
+        offsets = keep.tile([P, I // LIST_ROWS], U16, name="offsets")
         hid_raw = keep.tile([P, PACK, Q], F32, name="hid_raw")
         hid_bf = keep.tile([P, Q, PACK], BF16, name="hid_bf", align_bytes=64)
         hid_codes = keep.tile([P, Q], U32, name="hid_codes", align_bytes=64)
         hid_scales = keep.tile([P, Q], U8, name="hid_scales", align_bytes=64)
-        voc_planes = keep.tile([P, N], U8, name="voc_planes", align_bytes=64)
+        voc_scale_sb = keep.tile([P, N], U8, name="voc_scale_sb", align_bytes=64)
         voc_codes = [keep.tile([P, N], U32, name="voc_codes%d" % c, align_bytes=64) for c in range(CHUNKS)]
         lpo_sb = keep.tile([P, I], F32, name="lpo_sb")
         adv_sb = keep.tile([P, I], F32, name="adv_sb")
@@ -46,27 +57,29 @@ def tile_attend_bpolicyratio_heads_kernel(tc, hid, voc_words, voc_scales, lpo, a
         picked = keep.tile([P, I], F32, name="picked")
         ratio = keep.tile([P, I], F32, name="ratio")
         gain = keep.tile([P, I], F32, name="gain")
-        chunk_max = keep.tile([P, CHUNKS], F32, name="chunk_max")
-        neg_max = keep.tile([P, 3], F32, name="neg_max")
-        group_sum = keep.tile([P, 3], F32, name="group_sum")
-        rescale = keep.tile([P, 3], F32, name="rescale")
-        weighted = keep.tile([P, 3], F32, name="weighted")
+        piece_max = keep.tile([P, len(SCORE_PIECES)], F32, name="piece_max")
+        neg_shift = keep.tile([P, GROUPS], F32, name="neg_shift")
+        group_sum = keep.tile([P, GROUPS], F32, name="group_sum")
+        rescale = keep.tile([P, GROUPS], F32, name="rescale")
+        weighted = keep.tile([P, GROUPS], F32, name="weighted")
         total = keep.tile([P, 1], F32, name="total")
         inv_total = keep.tile([P, 1], F32, name="inv_total")
-        neg_share = keep.tile([P, 3], F32, name="neg_share")
+        neg_share = keep.tile([P, GROUPS], F32, name="neg_share")
         gain_sum = keep.tile([P, 2], F32, name="gain_sum")
-        coef_part = keep.tile([P, 3], F32, name="coef_part")
-        coef = keep.tile([P, 3], F32, name="coef")
+        factor_part = keep.tile([P, GROUPS], F32, name="factor_part")
+        factor = keep.tile([P, GROUPS], F32, name="factor")
         identity = keep.tile([P, P], F32, name="identity")
 
         make_identity(nc, identity[:])
         nc.vector.memset(placed[:], 0.0)
 
-        nc.sync.dma_start(out=hid_raw[:], in_=hid.rearrange("(p j) q -> p j q", j=PACK))
-        for g in range(4):
-            nc.scalar.dma_start(
-                out=voc_planes[32 * g : 32 * g + 16, :].bitcast(I32),
-                in_=voc_scales[0][4 * g : 4 * g + 4, :].rearrange("r (c n) -> c r n", c=CHUNKS).bitcast(I32),
+        nc.sync.dma_start(out=hid_raw[:], in_=hid.rearrange("(p t) q -> p t q", t=PACK))
+        for g in range(P // QUADRANT):
+            nc.sync.dma_start(
+                out=voc_scale_sb[QUADRANT * g : QUADRANT * g + CHUNKS * SCALE_ROWS, :].bitcast(I32),
+                in_=voc_scales[0][SCALE_ROWS * g : SCALE_ROWS * (g + 1), :]
+                .rearrange("r (c n) -> c r n", c=CHUNKS)
+                .bitcast(I32),
             )
         words = voc_words[0].rearrange("p n t -> p (n t)")
         for c in range(CHUNKS):
@@ -80,55 +93,67 @@ def tile_attend_bpolicyratio_heads_kernel(tc, hid, voc_words, voc_scales, lpo, a
         for h in range(2):
             nc.sync.dma_start(out=old_sb[h][:], in_=old[:, h * HALF : (h + 1) * HALF])
 
-        for copy, rows in ((nc.vector.tensor_copy, slice(0, Q // 2)), (nc.scalar.copy, slice(Q // 2, Q))):
+        for copy, cols in ((nc.vector.tensor_copy, slice(0, Q // 2)), (nc.scalar.copy, slice(Q // 2, Q))):
             copy(
-                hid_bf[:, rows, :].rearrange("p (c i) j -> p c j i", i=4),
-                hid_raw[:, :, rows].rearrange("p j (c i) -> p c j i", i=4),
+                hid_bf[:, cols, :].rearrange("p (c i) t -> p c t i", i=LINE),
+                hid_raw[:, :, cols].rearrange("p t (c i) -> p c t i", i=LINE),
             )
         nc.vector.quantize_mx(
             out=hid_codes[:].bitcast(FP8X4),
             scales=hid_scales[:],
-            in_=hid_bf[:].rearrange("p q j -> p (q j)"),
+            in_=hid_bf[:].rearrange("p q t -> p (q t)"),
         )
 
-        for c in range(CHUNKS):
-            bank = psum.tile([P, N], F32, name="bank%d" % c, tag="bank%d" % c)
+        def exp_group(g, first_piece, end_piece):
+            nc.vector.tensor_reduce(
+                out=neg_shift[:, g : g + 1], in_=piece_max[:, first_piece:end_piece], axis=mybir.AxisListType.X,
+                op=ALU.max, negate=True,
+            )
+            nc.scalar.activation(
+                out=probs[:, g * N : (g + 1) * N], in_=scores[:, g * N : (g + 1) * N], func=ACT.Exp,
+                bias=neg_shift[:, g : g + 1], accum_out=group_sum[:, g : g + 1],
+            )
+
+        def score_piece(k):
+            first, width = SCORE_PIECES[k]
+            c = first // N
+            cols = slice(first - c * N, first - c * N + width)
+            bank = psum.tile([P, width], F32, name="bank%d" % k, tag="bank%d" % k)
             nc.tensor.matmul_mx(
                 out=bank[:],
                 lhsT=hid_codes[:].bitcast(FP8X4),
                 lhsT_scale=hid_scales[:],
-                rhs=voc_codes[c][:].bitcast(FP8X4),
-                rhs_scale=voc_planes[4 * c : P, :],
+                rhs=voc_codes[c][:, cols].bitcast(FP8X4),
+                rhs_scale=voc_scale_sb[SCALE_ROWS * c : P, cols],
                 start=True,
                 stop=True,
             )
             nc.vector.tensor_scalar(
-                out=scores[:, c * N : (c + 1) * N],
+                out=scores[:, first : first + width],
                 in0=bank[:],
                 scalar1=1.0,
                 scalar2=None,
                 op0=ALU.mult,
                 op1=ALU.max,
-                accum_out=chunk_max[:, c : c + 1],
+                accum_out=piece_max[:, k : k + 1],
             )
-            if 1 <= c <= 2:
-                g = c - 1
-                nc.vector.tensor_scalar(
-                    out=neg_max[:, g : g + 1], in0=chunk_max[:, g : g + 1], scalar1=-1.0, scalar2=None, op0=ALU.mult
-                )
-                nc.scalar.activation(
-                    out=probs[:, g * N : (g + 1) * N], in_=scores[:, g * N : (g + 1) * N], func=ACT.Exp,
-                    bias=neg_max[:, g : g + 1], accum_out=group_sum[:, g : g + 1],
-                )
 
-        nc.vector.tensor_reduce(
-            out=neg_max[:, 2:3], in_=chunk_max[:], axis=mybir.AxisListType.X, op=ALU.max, negate=True
-        )
+        score_piece(0)
+        score_piece(1)
+        score_piece(2)
+        exp_group(0, 0, 2)
+        score_piece(3)
+        exp_group(1, 2, 3)
+        score_piece(4)
+        score_piece(5)
+
+        neg_row_max = neg_shift[:, LAST_GROUP:GROUPS]
+        nc.vector.tensor_reduce(out=neg_row_max, in_=piece_max[:], axis=mybir.AxisListType.X, op=ALU.max, negate=True)
         nc.vector.tensor_tensor(picked[:], scores[:].indirect(offsets[:]), lpo_sb[:], ALU.subtract)
-        nc.scalar.activation(out=rescale[:], in_=neg_max[:], func=ACT.Exp, bias=neg_max[:, 2:3], scale=-1.0)
+        nc.scalar.activation(out=rescale[:], in_=neg_shift[:], func=ACT.Exp, bias=neg_row_max, scale=-1.0)
         nc.scalar.activation(
-            out=probs[:, HALF:V], in_=scores[:, HALF:V], func=ACT.Exp,
-            bias=neg_max[:, 2:3], accum_out=group_sum[:, 2:3],
+            out=probs[:, LAST_GROUP * N : V], in_=scores[:, LAST_GROUP * N : V], func=ACT.Exp,
+            bias=neg_row_max, accum_out=group_sum[:, LAST_GROUP:GROUPS],
         )
         nc.vector.scalar_tensor_tensor(
             out=weighted[:], in0=group_sum[:], scalar=1.0, in1=rescale[:], op0=ALU.mult, op1=ALU.mult,
@@ -140,31 +165,35 @@ def tile_attend_bpolicyratio_heads_kernel(tc, hid, voc_words, voc_scales, lpo, a
         )
         for s in range(2):
             slots = slice(s * I // 2, (s + 1) * I // 2)
-            nc.scalar.activation(out=ratio[:, slots], in_=picked[:, slots], func=ACT.Exp, bias=neg_max[:, 2:3])
+            nc.scalar.activation(out=ratio[:, slots], in_=picked[:, slots], func=ACT.Exp, bias=neg_row_max)
             nc.vector.scalar_tensor_tensor(
                 out=gain[:, slots], in0=ratio[:, slots], scalar=inv_total[:], in1=adv_sb[:, slots],
                 op0=ALU.mult, op1=ALU.mult, accum_out=gain_sum[:, s : s + 1],
             )
-        nc.scalar.activation(out=coef_part[:], in_=neg_share[:], func=ACT.Copy, scale=gain_sum[:, 0:1])
-        for g in range(3):
+        nc.scalar.activation(out=factor_part[:], in_=neg_share[:], func=ACT.Copy, scale=gain_sum[:, 0:1])
+        for g in range(GROUPS):
             nc.scalar.activation(
-                out=coef[:, g : g + 1], in_=neg_share[:, g : g + 1], func=ACT.Identity,
-                scale=gain_sum[:, 1:2], bias=coef_part[:, g : g + 1],
+                out=factor[:, g : g + 1], in_=neg_share[:, g : g + 1], func=ACT.Identity,
+                scale=gain_sum[:, 1:2], bias=factor_part[:, g : g + 1],
             )
         nc.vector.tensor_copy(placed[:].indirect(offsets[:]), gain[:])
 
-        def old_cols(c0, w):
-            h = c0 // HALF
-            return old_sb[h][:, c0 - h * HALF : c0 - h * HALF + w]
+        def old_cols(first, width):
+            h = first // HALF
+            return old_sb[h][:, first - h * HALF : first - h * HALF + width]
 
-        def coef_of(c):
-            return coef[:, min(c, 2) : min(c, 2) + 1]
+        def scale_probs(first, width):
+            g = min(first // N, LAST_GROUP)
+            scaled = keep.tile([P, width], F32, name="scaled%d" % first)
+            nc.scalar.activation(
+                out=scaled[:], in_=probs[:, first : first + width], func=ACT.Copy, scale=factor[:, g : g + 1]
+            )
+            return scaled
 
-        widths = TURNED_WIDTHS
         turned = []
-        for c in range(len(widths)):
-            acc = psum.tile([P, widths[c]], F32, name="acc%d" % c)
-            for b in range(widths[c] // P):
+        for c, width in enumerate(TURNED_WIDTHS):
+            acc = psum.tile([P, width], F32, name="acc%d" % c, tag=ACC_TAGS[c])
+            for b in range(width // P):
                 nc.tensor.matmul(
                     acc[:, b * P : (b + 1) * P], lhsT=old_cols(c * N + b * P, P), rhs=identity[:],
                     start=(b == 0), stop=False, is_transpose=True,
@@ -172,11 +201,8 @@ def tile_attend_bpolicyratio_heads_kernel(tc, hid, voc_words, voc_scales, lpo, a
             turned.append(acc)
 
         def scale_and_turn(c):
-            blocks = widths[c] // P
-            scaled = keep.tile([P, widths[c]], F32, name="scaled%d" % c)
-            nc.scalar.activation(
-                out=scaled[:], in_=probs[:, c * N : c * N + widths[c]], func=ACT.Copy, scale=coef_of(c)
-            )
+            blocks = TURNED_WIDTHS[c] // P
+            scaled = scale_probs(c * N, TURNED_WIDTHS[c])
             for b in range(blocks):
                 nc.tensor.matmul(
                     turned[c][:, b * P : (b + 1) * P], lhsT=scaled[:, b * P : (b + 1) * P], rhs=identity[:],
@@ -184,37 +210,37 @@ def tile_attend_bpolicyratio_heads_kernel(tc, hid, voc_words, voc_scales, lpo, a
                 )
 
         def turn_back(c):
-            staged = keep.tile([P, widths[c]], F32, name="staged%d" % c)
+            width = TURNED_WIDTHS[c]
+            staged = keep.tile([P, width], F32, name="staged%d" % c)
             nc.scalar.copy(staged[:], turned[c][:])
-            back = psum.tile([P, widths[c]], F32, name="back%d" % c, tag="bank%d" % c)
-            for b in range(widths[c] // P):
-                nc.tensor.transpose(back[:, b * P : (b + 1) * P], staged[:, b * P : (b + 1) * P], identity[:])
-            return back
+            dense = psum.tile([P, width], F32, name="dense%d" % c, tag="bank%d" % (c + 1))
+            for b in range(width // P):
+                nc.tensor.transpose(dense[:, b * P : (b + 1) * P], staged[:, b * P : (b + 1) * P], identity[:])
+            return dense
 
-        def finish(dense, c0, w):
-            result = keep.tile([P, w], F32, name="result%d" % c0)
-            nc.vector.tensor_tensor(result[:], dense, placed[:, c0 : c0 + w], ALU.add)
-            nc.sync.dma_start(out=out[:, c0 : c0 + w], in_=result[:])
+        def add_on_gpsimd(first, width):
+            scaled = scale_probs(first, width)
+            dense = keep.tile([P, width], F32, name="dense_at%d" % first)
+            nc.gpsimd.tensor_tensor(dense[:], scaled[:], old_cols(first, width), ALU.add)
+            return dense
 
-        def add_on_gpsimd(c0, w):
-            scaled = keep.tile([P, w], F32, name="scaled_at%d" % c0)
-            nc.scalar.activation(out=scaled[:], in_=probs[:, c0 : c0 + w], func=ACT.Copy, scale=coef_of(2))
-            summed = keep.tile([P, w], F32, name="summed_at%d" % c0)
-            nc.gpsimd.tensor_tensor(summed[:], scaled[:], old_cols(c0, w), ALU.add)
-            return summed
+        def finish(dense, first, width):
+            result = keep.tile([P, width], F32, name="result%d" % first)
+            nc.vector.tensor_tensor(result[:], dense, placed[:, first : first + width], ALU.add)
+            nc.sync.dma_start(out=out[:, first : first + width], in_=result[:])
 
         scale_and_turn(0)
         scale_and_turn(1)
-        back0 = turn_back(0)
-        summed_a = add_on_gpsimd(1280, 512)
+        dense0 = turn_back(0)
+        dense_gpsimd_first = add_on_gpsimd(GPSIMD_START, GPSIMD_FIRST)
         scale_and_turn(2)
-        back1 = turn_back(1)
-        summed_b = add_on_gpsimd(1792, 256)
-        back2 = turn_back(2)
+        dense1 = turn_back(1)
+        dense_gpsimd_last = add_on_gpsimd(V - GPSIMD_LAST, GPSIMD_LAST)
+        dense2 = turn_back(2)
 
-        finish(back0[:, 0:256], 0, 256)
-        finish(back0[:, 256:512], 256, 256)
-        finish(back1[:], 512, 512)
-        finish(back2[:], 1024, 256)
-        finish(summed_a[:], 1280, 512)
-        finish(summed_b[:], 1792, 256)
+        finish(dense0[:, 0 : N // 2], 0, N // 2)
+        finish(dense0[:, N // 2 : N], N // 2, N // 2)
+        finish(dense1[:], N, N)
+        finish(dense2[:], 2 * N, TURNED_WIDTHS[2])
+        finish(dense_gpsimd_first[:], GPSIMD_START, GPSIMD_FIRST)
+        finish(dense_gpsimd_last[:], V - GPSIMD_LAST, GPSIMD_LAST)

from contextlib import ExitStack

import concourse.mybir as mybir
from concourse.masks import make_identity

D, V, Q, I = 512, 2048, 128, 512
FLOPS = 2 * D * V * Q

F32 = mybir.dt.float32
BF16 = mybir.dt.bfloat16
I32 = mybir.dt.int32
U32 = mybir.dt.uint32
U16 = mybir.dt.uint16
U8 = mybir.dt.uint8
FP8X4 = mybir.dt.float8_e4m3fn_x4
ALU = mybir.AluOpType
ACT = mybir.ActivationFunctionType

P = 128
PACK = 4
LIST_ROWS = 16
QUADRANT = 32
SCALE_ROWS = 4
LINE = 4
N = 512
CHUNKS = V // N
HALF = V // 2
SCORE_PIECES = ((0, N // 2), (N // 2, N // 2), (N, N), (2 * N, N), (3 * N, N // 2), (3 * N + N // 2, N // 2))
GROUPS = 3
LAST_GROUP = GROUPS - 1
TURNED_WIDTHS = (N, N, N // 2)
ACC_TAGS = ("acc0", "acc1", "bank0")
GPSIMD_START = sum(TURNED_WIDTHS)
GPSIMD_LAST = 256
GPSIMD_FIRST = V - GPSIMD_START - GPSIMD_LAST


def tile_attend_bpolicyratio_heads_kernel(tc, hid, voc_words, voc_scales, lpo, adv, old, offs, out):
    nc = tc.nc
    with ExitStack() as ctx:
        keep = ctx.enter_context(tc.tile_pool(name="keep", bufs=1))
        psum = ctx.enter_context(tc.psum_pool(name="psum", bufs=1))

        offsets = keep.tile([P, I // LIST_ROWS], U16, name="offsets")
        hid_raw = keep.tile([P, PACK, Q], F32, name="hid_raw")
        hid_bf = keep.tile([P, Q, PACK], BF16, name="hid_bf", align_bytes=64)
        hid_codes = keep.tile([P, Q], U32, name="hid_codes", align_bytes=64)
        hid_scales = keep.tile([P, Q], U8, name="hid_scales", align_bytes=64)
        voc_scale_sb = keep.tile([P, N], U8, name="voc_scale_sb", align_bytes=64)
        voc_codes = [keep.tile([P, N], U32, name="voc_codes%d" % c, align_bytes=64) for c in range(CHUNKS)]
        lpo_sb = keep.tile([P, I], F32, name="lpo_sb")
        adv_sb = keep.tile([P, I], F32, name="adv_sb")
        old_sb = [keep.tile([P, HALF], F32, name="old_sb%d" % h) for h in range(2)]
        scores = keep.tile([P, V], F32, name="scores")
        probs = keep.tile([P, V], F32, name="probs")
        placed = keep.tile([P, V], F32, name="placed")
        picked = keep.tile([P, I], F32, name="picked")
        ratio = keep.tile([P, I], F32, name="ratio")
        gain = keep.tile([P, I], F32, name="gain")
        piece_max = keep.tile([P, len(SCORE_PIECES)], F32, name="piece_max")
        neg_shift = keep.tile([P, GROUPS], F32, name="neg_shift")
        group_sum = keep.tile([P, GROUPS], F32, name="group_sum")
        rescale = keep.tile([P, GROUPS], F32, name="rescale")
        weighted = keep.tile([P, GROUPS], F32, name="weighted")
        total = keep.tile([P, 1], F32, name="total")
        inv_total = keep.tile([P, 1], F32, name="inv_total")
        neg_share = keep.tile([P, GROUPS], F32, name="neg_share")
        gain_sum = keep.tile([P, 2], F32, name="gain_sum")
        factor_part = keep.tile([P, GROUPS], F32, name="factor_part")
        factor = keep.tile([P, GROUPS], F32, name="factor")
        identity = keep.tile([P, P], F32, name="identity")

        make_identity(nc, identity[:])
        nc.vector.memset(placed[:], 0.0)

        nc.sync.dma_start(out=hid_raw[:], in_=hid.rearrange("(p t) q -> p t q", t=PACK))
        for g in range(P // QUADRANT):
            nc.sync.dma_start(
                out=voc_scale_sb[QUADRANT * g : QUADRANT * g + CHUNKS * SCALE_ROWS, :].bitcast(I32),
                in_=voc_scales[0][SCALE_ROWS * g : SCALE_ROWS * (g + 1), :]
                .rearrange("r (c n) -> c r n", c=CHUNKS)
                .bitcast(I32),
            )
        words = voc_words[0].rearrange("p n t -> p (n t)")
        for c in range(CHUNKS):
            nc.sync.dma_start(
                out=voc_codes[c][:].bitcast(I32),
                in_=words[:, c * N * PACK : (c + 1) * N * PACK].bitcast(I32),
            )
        nc.sync.dma_start(offsets[:], offs)
        nc.sync.dma_start(out=lpo_sb[:], in_=lpo)
        nc.sync.dma_start(out=adv_sb[:], in_=adv)
        for h in range(2):
            nc.sync.dma_start(out=old_sb[h][:], in_=old[:, h * HALF : (h + 1) * HALF])

        for copy, cols in ((nc.vector.tensor_copy, slice(0, Q // 2)), (nc.scalar.copy, slice(Q // 2, Q))):
            copy(
                hid_bf[:, cols, :].rearrange("p (c i) t -> p c t i", i=LINE),
                hid_raw[:, :, cols].rearrange("p t (c i) -> p c t i", i=LINE),
            )
        nc.vector.quantize_mx(
            out=hid_codes[:].bitcast(FP8X4),
            scales=hid_scales[:],
            in_=hid_bf[:].rearrange("p q t -> p (q t)"),
        )

        def exp_group(g, first_piece, end_piece):
            nc.vector.tensor_reduce(
                out=neg_shift[:, g : g + 1], in_=piece_max[:, first_piece:end_piece], axis=mybir.AxisListType.X,
                op=ALU.max, negate=True,
            )
            nc.scalar.activation(
                out=probs[:, g * N : (g + 1) * N], in_=scores[:, g * N : (g + 1) * N], func=ACT.Exp,
                bias=neg_shift[:, g : g + 1], accum_out=group_sum[:, g : g + 1],
            )

        def score_piece(k):
            first, width = SCORE_PIECES[k]
            c = first // N
            cols = slice(first - c * N, first - c * N + width)
            bank = psum.tile([P, width], F32, name="bank%d" % k, tag="bank%d" % k)
            nc.tensor.matmul_mx(
                out=bank[:],
                lhsT=hid_codes[:].bitcast(FP8X4),
                lhsT_scale=hid_scales[:],
                rhs=voc_codes[c][:, cols].bitcast(FP8X4),
                rhs_scale=voc_scale_sb[SCALE_ROWS * c : P, cols],
                start=True,
                stop=True,
            )
            nc.vector.tensor_scalar(
                out=scores[:, first : first + width],
                in0=bank[:],
                scalar1=1.0,
                scalar2=None,
                op0=ALU.mult,
                op1=ALU.max,
                accum_out=piece_max[:, k : k + 1],
            )

        score_piece(0)
        score_piece(1)
        score_piece(2)
        exp_group(0, 0, 2)
        score_piece(3)
        exp_group(1, 2, 3)
        score_piece(4)
        score_piece(5)

        neg_row_max = neg_shift[:, LAST_GROUP:GROUPS]
        nc.vector.tensor_reduce(out=neg_row_max, in_=piece_max[:], axis=mybir.AxisListType.X, op=ALU.max, negate=True)
        nc.vector.tensor_tensor(picked[:], scores[:].indirect(offsets[:]), lpo_sb[:], ALU.subtract)
        nc.scalar.activation(out=rescale[:], in_=neg_shift[:], func=ACT.Exp, bias=neg_row_max, scale=-1.0)
        nc.scalar.activation(
            out=probs[:, LAST_GROUP * N : V], in_=scores[:, LAST_GROUP * N : V], func=ACT.Exp,
            bias=neg_row_max, accum_out=group_sum[:, LAST_GROUP:GROUPS],
        )
        nc.vector.scalar_tensor_tensor(
            out=weighted[:], in0=group_sum[:], scalar=1.0, in1=rescale[:], op0=ALU.mult, op1=ALU.mult,
            accum_out=total[:],
        )
        nc.vector.reciprocal(inv_total[:], total[:])
        nc.vector.tensor_scalar(
            out=neg_share[:], in0=rescale[:], scalar1=inv_total[:], scalar2=-1.0, op0=ALU.mult, op1=ALU.mult
        )
        for s in range(2):
            slots = slice(s * I // 2, (s + 1) * I // 2)
            nc.scalar.activation(out=ratio[:, slots], in_=picked[:, slots], func=ACT.Exp, bias=neg_row_max)
            nc.vector.scalar_tensor_tensor(
                out=gain[:, slots], in0=ratio[:, slots], scalar=inv_total[:], in1=adv_sb[:, slots],
                op0=ALU.mult, op1=ALU.mult, accum_out=gain_sum[:, s : s + 1],
            )
        nc.scalar.activation(out=factor_part[:], in_=neg_share[:], func=ACT.Copy, scale=gain_sum[:, 0:1])
        for g in range(GROUPS):
            nc.scalar.activation(
                out=factor[:, g : g + 1], in_=neg_share[:, g : g + 1], func=ACT.Identity,
                scale=gain_sum[:, 1:2], bias=factor_part[:, g : g + 1],
            )
        nc.vector.tensor_copy(placed[:].indirect(offsets[:]), gain[:])

        def old_cols(first, width):
            h = first // HALF
            return old_sb[h][:, first - h * HALF : first - h * HALF + width]

        def scale_probs(first, width):
            g = min(first // N, LAST_GROUP)
            scaled = keep.tile([P, width], F32, name="scaled%d" % first)
            nc.scalar.activation(
                out=scaled[:], in_=probs[:, first : first + width], func=ACT.Copy, scale=factor[:, g : g + 1]
            )
            return scaled

        turned = []
        for c, width in enumerate(TURNED_WIDTHS):
            acc = psum.tile([P, width], F32, name="acc%d" % c, tag=ACC_TAGS[c])
            for b in range(width // P):
                nc.tensor.matmul(
                    acc[:, b * P : (b + 1) * P], lhsT=old_cols(c * N + b * P, P), rhs=identity[:],
                    start=(b == 0), stop=False, is_transpose=True,
                )
            turned.append(acc)

        def scale_and_turn(c):
            blocks = TURNED_WIDTHS[c] // P
            scaled = scale_probs(c * N, TURNED_WIDTHS[c])
            for b in range(blocks):
                nc.tensor.matmul(
                    turned[c][:, b * P : (b + 1) * P], lhsT=scaled[:, b * P : (b + 1) * P], rhs=identity[:],
                    start=False, stop=(b == blocks - 1), is_transpose=True,
                )

        def turn_back(c):
            width = TURNED_WIDTHS[c]
            staged = keep.tile([P, width], F32, name="staged%d" % c)
            nc.scalar.copy(staged[:], turned[c][:])
            dense = psum.tile([P, width], F32, name="dense%d" % c, tag="bank%d" % (c + 1))
            for b in range(width // P):
                nc.tensor.transpose(dense[:, b * P : (b + 1) * P], staged[:, b * P : (b + 1) * P], identity[:])
            return dense

        def add_on_gpsimd(first, width):
            scaled = scale_probs(first, width)
            dense = keep.tile([P, width], F32, name="dense_at%d" % first)
            nc.gpsimd.tensor_tensor(dense[:], scaled[:], old_cols(first, width), ALU.add)
            return dense

        def finish(dense, first, width):
            result = keep.tile([P, width], F32, name="result%d" % first)
            nc.vector.tensor_tensor(result[:], dense, placed[:, first : first + width], ALU.add)
            nc.sync.dma_start(out=out[:, first : first + width], in_=result[:])

        scale_and_turn(0)
        scale_and_turn(1)
        dense0 = turn_back(0)
        dense_gpsimd_first = add_on_gpsimd(GPSIMD_START, GPSIMD_FIRST)
        scale_and_turn(2)
        dense1 = turn_back(1)
        dense_gpsimd_last = add_on_gpsimd(V - GPSIMD_LAST, GPSIMD_LAST)
        dense2 = turn_back(2)

        finish(dense0[:, 0 : N // 2], 0, N // 2)
        finish(dense0[:, N // 2 : N], N // 2, N // 2)
        finish(dense1[:], N, N)
        finish(dense2[:], 2 * N, TURNED_WIDTHS[2])
        finish(dense_gpsimd_first[:], GPSIMD_START, GPSIMD_FIRST)
        finish(dense_gpsimd_last[:], V - GPSIMD_LAST, GPSIMD_LAST)
